import numpy as np
import ml_dtypes


def mxq(x, axis, fmt="e4m3"):
    dtype, down = {"e4m3": (ml_dtypes.float8_e4m3fn, 7), "e5m2": (ml_dtypes.float8_e5m2, 14)}[fmt]
    v = np.moveaxis(np.asarray(x, np.float32).astype(ml_dtypes.bfloat16).astype(np.float64), axis, -1)
    blocks = v.reshape(v.shape[:-1] + (-1, 32))
    amax = np.abs(blocks).max(-1, keepdims=True)
    byte = np.maximum(np.where(amax > 0, np.frexp(amax)[1] - 1 + 127, 0) - down, 1)
    scale = np.exp2(byte - 127.0)
    codes = (blocks / scale).astype(np.float32).astype(dtype).astype(np.float64)
    return np.moveaxis((codes * scale).reshape(v.shape), -1, axis)


WIDE = False


def mx_kscale(k):
    if not WIDE:
        return np.ones(k)
    levels = np.array([10, -10, 5, -5, 0])
    if k % 512:
        return np.exp2(np.random.permutation(np.resize(levels, k // 32))).repeat(32)
    a = np.empty((k // 512, 16))
    for p in range(k // 512):
        a[p, :8] = np.random.permutation(np.resize(levels, 8))
        for g in range(8):
            far = levels[np.abs(levels - a[p, g]) >= 10]
            a[p, g + 8] = far[np.random.randint(len(far))]
    return np.exp2(a.ravel()).repeat(32)


def f64(x):
    return np.asarray(x).astype(np.float64)


def striped(idx):
    return np.tile(idx.reshape(-1, 16).T, (8, 1)).astype(np.uint16)


def unstriped(offs):
    return offs[:16].T.reshape(-1).astype(np.int64)


def striped8(idx):
    return np.concatenate([x.reshape(-1, 16).T for x in idx]).astype(np.uint16)


def runs(offs, k):
    lists = np.stack([offs[16 * r : 16 * r + 16].T.reshape(-1) for r in range(8)]).astype(np.int64)
    return lists[np.arange(k) % 512 // 64]


def pack_weight(w):
    k, n = w.shape
    w = f64(np.asarray(w, np.float32).astype(ml_dtypes.bfloat16)).reshape(k // 32, 32, n)
    amax = np.abs(w).max(1)
    byte = np.clip(np.where(amax > 0, np.frexp(amax)[1] - 1 + 127 - 7, 1), 1, 254)
    scaled = (w * np.exp2(127.0 - byte)[:, None, :]).reshape(k, n).astype(np.float32)
    words = np.ascontiguousarray(scaled.reshape(k // 512, 128, 4, n).transpose(0, 1, 3, 2)).astype(ml_dtypes.float8_e4m3fn).view(np.uint8)
    return words, np.ascontiguousarray(byte.astype(np.uint8).reshape(k // 512, 16, n))


def unpack_weight(words, scales):
    g, p, n, _ = words.shape
    vals = np.ascontiguousarray(words).view(ml_dtypes.float8_e4m3fn).astype(np.float64) * np.repeat(np.exp2(scales.astype(np.float64) - 127.0), 8, axis=1)[..., None]
    return vals.transpose(0, 1, 3, 2).reshape(g * 512, n)


def sigmoid(v):
    return 1.0 / (1.0 + np.exp(-np.maximum(v, -700.0)))

def planes(y):
    n, m = y.shape
    v = y.astype(np.float32).astype(ml_dtypes.bfloat16).astype(np.float64).reshape(n // 32, 32, m)
    top = np.abs(v).max(1)
    byte = np.clip(np.where(top > 0, np.frexp(top)[1] - 1 + 127 - 7, 1), 1, 254)
    codes = (v * np.exp2(127.0 - byte)[:, None, :]).reshape(n, m).astype(np.float32).astype(ml_dtypes.float8_e4m3fn).view(np.uint8)
    words = codes.reshape(n // 512, 128, 4, m).transpose(0, 1, 3, 2)
    return np.ascontiguousarray(words), np.ascontiguousarray(byte.astype(np.uint8).reshape(n // 512, 16, m))


K, T, S, H, J, C = 512, 2048, 256, 512, 512, 512


def setup_inputs():
    n = np.random.standard_normal
    s = mx_kscale(K)[:, None]
    packed_xT = pack_weight(n((K, T)) * s)
    packed_w1 = pack_weight(n((K, H)) / np.sqrt(K) / s)
    return {
        "x_words": packed_xT[0],
        "x_scales": packed_xT[1],
        "w1_words": packed_w1[0],
        "w1_scales": packed_w1[1],
        "tab": n((H, J)).astype(np.float32),
        "gs": (np.random.uniform(0.5, 1.5, (K, 1)) / s).astype(np.float32),
        "gs2": (np.random.uniform(0.5, 1.5, (K, 1)) / s).astype(np.float32),
        "offs": striped(np.random.permutation(T)[:S]),
        "n1": striped(np.random.randint(0, J, S)),
        "n2": striped(np.random.permutation(S)),
        "n3": striped(np.random.permutation(S)),
        "n4": striped(np.random.permutation(S)),
        "ca": striped(np.random.permutation(T)[:C]),
        "cb": striped(np.random.permutation(T)[:C]),
        "n5": striped8(np.stack([np.random.permutation(S) for _ in range(8)])),
        "n6": striped8(np.stack([np.random.permutation(S) for _ in range(8)])),
    }


def reference(x_words, x_scales, w1_words, w1_scales, tab, gs, gs2, offs, n1, n2, n3, n4, ca, cb, n5, n6):
    x_ca = unpack_weight(x_words, x_scales)[:, unstriped(ca)]
    xq = unpack_weight(x_words, x_scales)[:, unstriped(offs)]
    y = unpack_weight(w1_words, w1_scales).T @ xq
    z = f64(gs) * (np.maximum(y + f64(tab)[:, unstriped(n1)], y[:, unstriped(n2)]))
    a = 0.0625 * ((x_ca.T @ mxq(z, 0, "e4m3")))
    x_cb = unpack_weight(x_words, x_scales)[:, unstriped(cb)]
    sq = (y) ** 2
    z2 = f64(gs2) * (y[:, unstriped(n4)] / (np.sqrt(sq + sq[:, unstriped(n3)] + 0.25)))
    b = 0.0625 * ((x_cb.T @ mxq(z2, 0, "e4m3")))
    out_0 = a * (sigmoid(b[np.arange(C)[:, None], runs(n6, C)])) - (0.5 * (a[np.arange(C)[:, None], runs(n5, C)]))
    return (out_0,) + planes(out_0)

@@ -1,0 +1,224 @@
+from contextlib import ExitStack
+
+import concourse.mybir as mybir
+
+K, T, S, H, J, C = 512, 2048, 256, 512, 512, 512
+FLOPS = 2 * K * H * S + 2 * 2 * K * C * S
+
+F32 = mybir.dt.float32
+BF16 = mybir.dt.bfloat16
+I32 = mybir.dt.int32
+U32 = mybir.dt.uint32
+U16 = mybir.dt.uint16
+U8 = mybir.dt.uint8
+FP8X4 = mybir.dt.float8_e4m3fn_x4
+ALU = mybir.AluOpType
+ACT = mybir.ActivationFunctionType
+
+P = 128
+PACK = 4
+QUADS = 4
+WIN = 352
+HALF = S // 2
+LIST_COL = 16
+
+
+def tile_picked_twocdgatebkindrms_none_po_kernel(
+    tc, x_words, x_scales, w1_words, w1_scales, tab, gs, gs2, offs, n1, n2, n3, n4, ca, cb, n5, n6, out_0, out_1, out_2
+):
+    nc = tc.nc
+    with ExitStack() as ctx:
+        keep = ctx.enter_context(tc.tile_pool(name="keep", bufs=1))
+        psum = ctx.enter_context(tc.psum_pool(name="psum", bufs=1))
+
+        def load_list(src, name):
+            lst = keep.tile(list(src.shape), U16, name=name)
+            nc.sync.dma_start(lst[:], src)
+            return lst
+
+        def load_scale_rows(queue, plane, src, q):
+            queue.dma_start(plane[32 * q : 32 * q + 4, :].bitcast(I32), src[0, 4 * q : 4 * q + 4, :].bitcast(I32))
+
+        def dealt(tile):
+            return tile[:].rearrange("p (t m) -> p m t", t=PACK)
+
+        def interleave(dst, src):
+            nc.vector.tensor_copy(
+                out=dst[:].rearrange("p (c i) t -> p c t i", i=4), in_=src[:].rearrange("p t (c i) -> p c t i", i=4)
+            )
+
+        xs = keep.tile([P, T], U8, name="xs", align_bytes=64)
+        w1s_raw = keep.tile([P, H], U8, name="w1s_raw", align_bytes=64)
+        nc.gpsimd.memset(xs[:].bitcast(I32), 0)
+        nc.gpsimd.memset(w1s_raw[:].bitcast(I32), 0)
+        xw = keep.tile([P, T], U32, name="xw", align_bytes=64)
+        w1w_raw = keep.tile([P, H], U32, name="w1w_raw", align_bytes=64)
+        tab_rows = tab.rearrange("(p t) j -> p t j", t=PACK)
+        tab_w = [keep.tile([P, J], F32, name="tab_win%d" % t) for t in range(PACK)]
+        gs_sb = keep.tile([P, PACK], F32, name="gs_sb")
+        gs2_sb = keep.tile([P, PACK], F32, name="gs2_sb")
+        offs_l = load_list(offs, "offs_l")
+        cb_l = load_list(cb, "cb_l")
+        load_scale_rows(nc.sync, xs, x_scales, 2)
+        load_scale_rows(nc.sync, xs, x_scales, 3)
+        nc.sync.dma_start(xw[:].bitcast(I32), x_words[0].rearrange("p n t -> p (n t)").bitcast(I32))
+        n1_l = load_list(n1, "n1_l")
+        n3_l = load_list(n3, "n3_l")
+        nc.sync.dma_start(w1w_raw[:].bitcast(I32), w1_words[0].rearrange("p n t -> p (n t)").bitcast(I32))
+        nc.sync.dma_start(tab_w[0][:], tab_rows[:, 0, :])
+        ca_l = load_list(ca, "ca_l")
+        n4_l = load_list(n4, "n4_l")
+        nc.sync.dma_start(tab_w[1][:], tab_rows[:, 1, :])
+        nc.sync.dma_start(tab_w[2][:], tab_rows[:, 2, :])
+        nc.sync.dma_start(tab_w[3][:], tab_rows[:, 3, :])
+        n2_l = load_list(n2, "n2_l")
+        nc.sync.dma_start(gs2_sb[:], gs2.rearrange("(p t) o -> p (t o)", t=PACK))
+        nc.sync.dma_start(gs_sb[:], gs.rearrange("(p t) o -> p (t o)", t=PACK))
+        n6_l = load_list(n6, "n6_l")
+        n5_l = load_list(n5, "n5_l")
+        load_scale_rows(nc.scalar, xs, x_scales, 0)
+        load_scale_rows(nc.scalar, xs, x_scales, 1)
+        load_scale_rows(nc.scalar, w1s_raw, w1_scales, 0)
+        load_scale_rows(nc.scalar, w1s_raw, w1_scales, 1)
+        load_scale_rows(nc.scalar, w1s_raw, w1_scales, 2)
+        load_scale_rows(nc.scalar, w1s_raw, w1_scales, 3)
+
+        y_w = [keep.tile([P, WIN], F32, name="y_win%d" % t) for t in range(PACK)]
+        sq_w = [keep.tile([P, WIN], F32, name="sq_win%d" % t) for t in range(PACK)]
+        b_w = [keep.tile([P, 2 * S], F32, name="b_win%d" % t) for t in range(PACK)]
+        for window in y_w + sq_w + b_w:
+            nc.vector.memset(window[:, S:], 0.0)
+
+        w1w = keep.tile([P, H], U32, name="w1w", align_bytes=64)
+        w1s = keep.tile([P, H], U8, name="w1s", align_bytes=64)
+        nc.vector.tensor_copy(out=dealt(w1s), in_=w1s_raw[:].rearrange("p (m t) -> p m t", t=PACK))
+        nc.scalar.copy(out=dealt(w1w), in_=w1w_raw[:].rearrange("p (m t) -> p m t", t=PACK))
+
+        xq_w = keep.tile([P, S], U32, name="xq_w", align_bytes=64)
+        xq_s = keep.tile([P, S], U8, name="xq_s", align_bytes=64)
+        nc.vector.tensor_copy(out=xq_w[:], in_=xw[:].indirect(offs_l[:]))
+        nc.vector.tensor_copy(out=xq_s[:], in_=xs[:].indirect(offs_l[:]))
+        y_ps = []
+        for t in range(PACK):
+            y_t = psum.tile([P, S], F32, name="y_ps%d" % t)
+            cols = slice(P * t, P * (t + 1))
+            nc.tensor.matmul_mx(
+                out=y_t[:], lhsT=w1w[:, cols].bitcast(FP8X4), lhsT_scale=w1s[:, cols],
+                rhs=xq_w[:].bitcast(FP8X4), rhs_scale=xq_s[:], start=True, stop=True,
+            )
+            y_ps.append(y_t)
+
+        def pick(window, dtype, lst, name, tag):
+            picked = keep.tile([P, C], dtype, name=name, tag=tag, align_bytes=64)
+            nc.vector.tensor_copy(out=dealt(picked), in_=window[:].indirect(lst[:]))
+            return picked
+
+        def score(picked, values, name, bank_tag):
+            grouped = keep.tile([P, S, PACK], BF16, name=name + "_bf", align_bytes=64)
+            codes = keep.tile([P, S], U32, name=name + "_codes", align_bytes=64)
+            scales = keep.tile([P, S], U8, name=name + "_scales", align_bytes=64)
+            interleave(grouped, values)
+            nc.vector.quantize_mx(out=codes[:].bitcast(FP8X4), scales=scales[:], in_=grouped[:].rearrange("p j t -> p (j t)"))
+            banks = [psum.tile([P, S], F32, name="%s_ps%d" % (name, t), tag="%s%d" % (bank_tag, t)) for t in range(PACK)]
+            for t in range(PACK):
+                cols = slice(P * t, P * (t + 1))
+                nc.tensor.matmul_mx(
+                    out=banks[t][:], lhsT=picked[0][:, cols].bitcast(FP8X4), lhsT_scale=picked[1][:, cols],
+                    rhs=codes[:].bitcast(FP8X4), rhs_scale=scales[:], start=True, stop=True,
+                )
+            return banks
+
+        x_cb = (pick(xw, U32, cb_l, "xcb_w", "xcb_w"), pick(xs, U8, cb_l, "xcb_s", "xcb_s"))
+        xca_s = pick(xs, U8, ca_l, "xca_s", "xca_s")
+        nc.scalar.activation(out=sq_w[0][:, :S], in_=y_ps[0][:], func=ACT.Square)
+        nc.scalar.copy(out=y_w[0][:, :S], in_=y_ps[0][:])
+        nc.scalar.activation(out=sq_w[1][:, :S], in_=y_ps[1][:], func=ACT.Square)
+        nc.scalar.copy(out=y_w[1][:, :S], in_=y_ps[1][:])
+        nc.scalar.activation(out=sq_w[2][:, :S], in_=y_ps[2][:], func=ACT.Square)
+        nc.scalar.copy(out=y_w[2][:, :S], in_=y_ps[2][:])
+        nc.scalar.activation(out=sq_w[3][:, :S], in_=y_ps[3][:], func=ACT.Square)
+        nc.scalar.copy(out=y_w[3][:, :S], in_=y_ps[3][:])
+        sq3 = keep.tile([P, PACK, S], F32, name="sq3", align_bytes=64)
+        ssum = keep.tile([P, PACK, S], F32, name="ssum")
+        rinv = keep.tile([P, PACK, S], F32, name="rinv")
+        y4 = keep.tile([P, PACK, S], F32, name="y4")
+        z2 = keep.tile([P, PACK, S], F32, name="z2")
+        tab1 = keep.tile([P, PACK, S], F32, name="tab1")
+        larger = keep.tile([P, PACK, S], F32, name="larger")
+        z = keep.tile([P, PACK, S], F32, name="z")
+        gate = [keep.tile([P, 2, S], F32, name="gate%d" % u) for u in range(2)]
+        gated = keep.tile([P, PACK, S], F32, name="gated")
+        a_w = [keep.tile([P, S], F32, name="a_win%d" % t) for t in range(PACK)]
+        res = [keep.tile([P, PACK, HALF], F32, name="res%d" % h) for h in range(2)]
+        res_bf = [keep.tile([P, HALF, PACK], BF16, name="res_bf%d" % h, align_bytes=64) for h in range(2)]
+        res_codes = keep.tile([P, S], U32, name="res_codes", align_bytes=64)
+        res_scales = keep.tile([P, S], U8, name="res_scales", align_bytes=64)
+        entries = [slice(h * HALF // LIST_COL, (h + 1) * HALF // LIST_COL) for h in range(2)]
+        nc.vector.tensor_copy(out=sq3[:, 0, :], in_=sq_w[0][:].indirect(n3_l[:]))
+        nc.vector.tensor_tensor(out=ssum[:, 0, :], in0=sq3[:, 0, :], in1=sq_w[0][:, :S], op=ALU.add)
+        nc.vector.tensor_copy(out=sq3[:, 1, :], in_=sq_w[1][:].indirect(n3_l[:]))
+        nc.vector.tensor_tensor(out=ssum[:, 1, :], in0=sq3[:, 1, :], in1=sq_w[1][:, :S], op=ALU.add)
+        nc.vector.tensor_copy(out=sq3[:, 2, :], in_=sq_w[2][:].indirect(n3_l[:]))
+        nc.vector.tensor_tensor(out=ssum[:, 2, :], in0=sq3[:, 2, :], in1=sq_w[2][:, :S], op=ALU.add)
+        nc.vector.tensor_copy(out=sq3[:, 3, :], in_=sq_w[3][:].indirect(n3_l[:]))
+        nc.vector.tensor_tensor(out=ssum[:, 3, :], in0=sq3[:, 3, :], in1=sq_w[3][:, :S], op=ALU.add)
+        x_ca = (pick(xw, U32, ca_l, "xca_w", "sq3"), xca_s)
+        for t in range(PACK):
+            nc.scalar.activation(out=y4[:, t, :], in_=y_w[t][:].indirect(n4_l[:]), func=ACT.Copy)
+        for u in range(2):
+            nc.scalar.activation(out=rinv[:, 2 * u : 2 * u + 2, :], in_=ssum[:, 2 * u : 2 * u + 2, :], func=ACT.Abs_reciprocal_sqrt, bias=0.25)
+        for t in range(PACK):
+            nc.vector.scalar_tensor_tensor(
+                out=z2[:, t, :], in0=y4[:, t, :], scalar=gs2_sb[:, t : t + 1], in1=rinv[:, t, :], op0=ALU.mult, op1=ALU.mult
+            )
+        b_ps = score(x_cb, z2, "b", "y_ps")
+        first = keep.tile([P, PACK, S], F32, name="first")
+        y2 = [keep.tile([P, 2, S], F32, name="y2_0"), keep.tile([P, 2, S], F32, name="y2_1")]
+        for t in range(PACK):
+            nc.scalar.activation(out=tab1[:, t, :], in_=tab_w[t][:].indirect(n1_l[:]), func=ACT.Copy)
+            nc.vector.tensor_tensor(out=first[:, t, :], in0=y_w[t][:, :S], in1=tab1[:, t, :], op=ALU.add)
+        nc.scalar.activation(out=y2[0][:, 0, :], in_=y_w[0][:].indirect(n2_l[:]), func=ACT.Copy)
+        nc.scalar.activation(out=y2[0][:, 1, :], in_=y_w[1][:].indirect(n2_l[:]), func=ACT.Copy)
+        nc.scalar.activation(out=y2[1][:, 0, :], in_=y_w[2][:].indirect(n2_l[:]), func=ACT.Copy)
+        nc.vector.tensor_copy(out=y2[1][:, 1, :], in_=y_w[3][:].indirect(n2_l[:]))
+        for u in range(2):
+            pair = slice(2 * u, 2 * u + 2)
+            nc.vector.tensor_tensor(out=larger[:, pair, :], in0=first[:, pair, :], in1=y2[u][:], op=ALU.max)
+        for t in range(PACK):
+            nc.vector.tensor_scalar(out=z[:, t, :], in0=larger[:, t, :], scalar1=gs_sb[:, t : t + 1], scalar2=None, op0=ALU.mult)
+        a_ps = score(x_ca, z, "a", "a_ps")
+        nc.scalar.activation(out=b_w[0][:, :S], in_=b_ps[0][:], func=ACT.Sigmoid, scale=0.0625)
+        nc.scalar.activation(out=b_w[1][:, :S], in_=b_ps[1][:], func=ACT.Sigmoid, scale=0.0625)
+        nc.scalar.activation(out=b_w[2][:, :S], in_=b_ps[2][:], func=ACT.Sigmoid, scale=0.0625)
+        nc.scalar.activation(out=b_w[3][:, :S], in_=b_ps[3][:], func=ACT.Sigmoid, scale=0.0625)
+        for t in range(PACK):
+            nc.scalar.activation(out=gate[t // 2][:, t % 2, :], in_=b_w[t][:].indirect(n6_l[:]), func=ACT.Copy)
+        nc.vector.tensor_scalar(out=a_w[0][:], in0=a_ps[0][:], scalar1=0.0625, scalar2=None, op0=ALU.mult)
+        nc.vector.tensor_scalar(out=a_w[1][:], in0=a_ps[1][:], scalar1=0.0625, scalar2=None, op0=ALU.mult)
+        nc.vector.tensor_scalar(out=a_w[2][:], in0=a_ps[2][:], scalar1=0.0625, scalar2=None, op0=ALU.mult)
+        nc.vector.tensor_scalar(out=a_w[3][:], in0=a_ps[3][:], scalar1=0.0625, scalar2=None, op0=ALU.mult)
+        for t in range(PACK):
+            nc.vector.scalar_tensor_tensor(
+                out=gated[:, t, :], in0=a_ps[t][:], scalar=0.0625, in1=gate[t // 2][:, t % 2, :], op0=ALU.mult, op1=ALU.mult
+            )
+        a5 = [keep.tile([P, PACK, HALF], F32, name="a5_0"), keep.tile([P, PACK, HALF], F32, name="a5_1", tag="gate0")]
+        out_rows = out_0.rearrange("(p t) j -> p t j", t=PACK)
+        out_words = out_1[0].rearrange("p n t -> p (n t)").bitcast(I32)
+        for h in range(2):
+            cols = slice(h * HALF, (h + 1) * HALF)
+            for u in range(2):
+                pair = slice(2 * u, 2 * u + 2)
+                for t in range(2 * u, 2 * u + 2):
+                    nc.scalar.activation(out=a5[h][:, t, :], in_=a_w[t][:].indirect(n5_l[:, entries[h]]), func=ACT.Copy)
+                nc.vector.scalar_tensor_tensor(
+                    out=res[h][:, pair, :], in0=a5[h][:, pair, :], scalar=-0.5, in1=gated[:, pair, cols], op0=ALU.mult, op1=ALU.add
+                )
+            nc.sync.dma_start(out_rows[:, :, cols], res[h][:])
+            interleave(res_bf[h], res[h])
+            nc.vector.quantize_mx(
+                out=res_codes[:, cols].bitcast(FP8X4), scales=res_scales[:, cols], in_=res_bf[h][:].rearrange("p j t -> p (j t)")
+            )
+            nc.sync.dma_start(out_words[:, cols], res_codes[:, cols].bitcast(I32))
+        for q in range(QUADS):
+            queue = nc.scalar if q % 2 else nc.sync
+            queue.dma_start(out_2[0, 4 * q : 4 * q + 4, :].bitcast(I32), res_scales[32 * q : 32 * q + 4, :].bitcast(I32))

@@ -1,6 +1,7 @@
 from contextlib import ExitStack
 
 import concourse.mybir as mybir
+from concourse.masks import make_identity
 
 K, T, S, H, J, C = 512, 2048, 256, 512, 512, 512
 FLOPS = 2 * K * H * S + 2 * 2 * K * C * S
@@ -16,11 +17,15 @@ ALU = mybir.AluOpType
 ACT = mybir.ActivationFunctionType
 
 P = 128
-PACK = 4
+SETS = 4
+PAIRS = SETS // 2
 QUADS = 4
-WIN = 352
 HALF = S // 2
-LIST_COL = 16
+LIST_ROWS = 16
+LINE = 4
+ONE_LIST_WINDOW = 352
+EIGHT_LIST_WINDOW = 2 * S
+SCORE_SCALE = 0.0625
 
 
 def tile_picked_twocdgatebkindrms_none_po_kernel(
@@ -36,187 +41,220 @@ def tile_picked_twocdgatebkindrms_none_po_kernel(
             nc.sync.dma_start(lst[:], src)
             return lst
 
-        def load_scale_rows(queue, plane, src, q):
-            queue.dma_start(plane[32 * q : 32 * q + 4, :].bitcast(I32), src[0, 4 * q : 4 * q + 4, :].bitcast(I32))
+        def load_scale_rows(queue, scale_tile, src, q):
+            queue.dma_start(scale_tile[32 * q : 32 * q + 4, :].bitcast(I32), src[0, 4 * q : 4 * q + 4, :].bitcast(I32))
+
+        def as_words(packed):
+            return packed[0].rearrange("p n t -> p (n t)").bitcast(I32)
+
+        def by_set(column):
+            return column.rearrange("(p t) o -> p (t o)", t=SETS)
 
         def dealt(tile):
-            return tile[:].rearrange("p (t m) -> p m t", t=PACK)
+            return tile[:].rearrange("p (t m) -> p m t", t=SETS)
 
         def interleave(dst, src):
             nc.vector.tensor_copy(
-                out=dst[:].rearrange("p (c i) t -> p c t i", i=4), in_=src[:].rearrange("p t (c i) -> p c t i", i=4)
+                out=dst[:].rearrange("p (c i) t -> p c t i", i=LINE), in_=src[:].rearrange("p t (c i) -> p c t i", i=LINE)
             )
 
         xs = keep.tile([P, T], U8, name="xs", align_bytes=64)
         w1s_raw = keep.tile([P, H], U8, name="w1s_raw", align_bytes=64)
         nc.gpsimd.memset(xs[:].bitcast(I32), 0)
         nc.gpsimd.memset(w1s_raw[:].bitcast(I32), 0)
+        ident = keep.tile([P, P], F32, name="ident")
+        make_identity(nc, ident[:])
+
         xw = keep.tile([P, T], U32, name="xw", align_bytes=64)
         w1w_raw = keep.tile([P, H], U32, name="w1w_raw", align_bytes=64)
-        tab_rows = tab.rearrange("(p t) j -> p t j", t=PACK)
-        tab_w = [keep.tile([P, J], F32, name="tab_win%d" % t) for t in range(PACK)]
-        gs_sb = keep.tile([P, PACK], F32, name="gs_sb")
-        gs2_sb = keep.tile([P, PACK], F32, name="gs2_sb")
+        tab_rows = tab.rearrange("(p t) j -> p t j", t=SETS)
+        tab_win = [keep.tile([P, J], F32, name="tab_win%d" % t) for t in range(SETS)]
+        gs_sb = keep.tile([P, SETS], F32, name="gs_sb")
+        gs2_sb = keep.tile([P, SETS], F32, name="gs2_sb")
         offs_l = load_list(offs, "offs_l")
         cb_l = load_list(cb, "cb_l")
-        load_scale_rows(nc.sync, xs, x_scales, 2)
-        load_scale_rows(nc.sync, xs, x_scales, 3)
-        nc.sync.dma_start(xw[:].bitcast(I32), x_words[0].rearrange("p n t -> p (n t)").bitcast(I32))
+        for q in range(QUADS // 2, QUADS):
+            load_scale_rows(nc.sync, xs, x_scales, q)
+        nc.sync.dma_start(xw[:].bitcast(I32), as_words(x_words))
+        for q in range(QUADS):
+            load_scale_rows(nc.sync, w1s_raw, w1_scales, q)
+        nc.sync.dma_start(w1w_raw[:].bitcast(I32), as_words(w1_words))
+        nc.sync.dma_start(tab_win[0][:], tab_rows[:, 0, :])
         n1_l = load_list(n1, "n1_l")
-        n3_l = load_list(n3, "n3_l")
-        nc.sync.dma_start(w1w_raw[:].bitcast(I32), w1_words[0].rearrange("p n t -> p (n t)").bitcast(I32))
-        nc.sync.dma_start(tab_w[0][:], tab_rows[:, 0, :])
         ca_l = load_list(ca, "ca_l")
+        n3_l = load_list(n3, "n3_l")
         n4_l = load_list(n4, "n4_l")
-        nc.sync.dma_start(tab_w[1][:], tab_rows[:, 1, :])
-        nc.sync.dma_start(tab_w[2][:], tab_rows[:, 2, :])
-        nc.sync.dma_start(tab_w[3][:], tab_rows[:, 3, :])
+        nc.sync.dma_start(tab_win[1][:], tab_rows[:, 1, :])
         n2_l = load_list(n2, "n2_l")
-        nc.sync.dma_start(gs2_sb[:], gs2.rearrange("(p t) o -> p (t o)", t=PACK))
-        nc.sync.dma_start(gs_sb[:], gs.rearrange("(p t) o -> p (t o)", t=PACK))
+        nc.sync.dma_start(gs2_sb[:], by_set(gs2))
+        for t in range(PAIRS, SETS):
+            nc.sync.dma_start(tab_win[t][:], tab_rows[:, t, :])
+        nc.sync.dma_start(gs_sb[:], by_set(gs))
         n6_l = load_list(n6, "n6_l")
         n5_l = load_list(n5, "n5_l")
-        load_scale_rows(nc.scalar, xs, x_scales, 0)
-        load_scale_rows(nc.scalar, xs, x_scales, 1)
-        load_scale_rows(nc.scalar, w1s_raw, w1_scales, 0)
-        load_scale_rows(nc.scalar, w1s_raw, w1_scales, 1)
-        load_scale_rows(nc.scalar, w1s_raw, w1_scales, 2)
-        load_scale_rows(nc.scalar, w1s_raw, w1_scales, 3)
+        for q in range(QUADS // 2):
+            load_scale_rows(nc.scalar, xs, x_scales, q)
 
-        y_w = [keep.tile([P, WIN], F32, name="y_win%d" % t) for t in range(PACK)]
-        sq_w = [keep.tile([P, WIN], F32, name="sq_win%d" % t) for t in range(PACK)]
-        b_w = [keep.tile([P, 2 * S], F32, name="b_win%d" % t) for t in range(PACK)]
-        for window in y_w + sq_w + b_w:
+        y_win = [keep.tile([P, ONE_LIST_WINDOW], F32, name="y_win%d" % t) for t in range(SETS)]
+        sq_win = [keep.tile([P, ONE_LIST_WINDOW], F32, name="sq_win%d" % t, align_bytes=64) for t in range(SETS)]
+        sig_win = [keep.tile([P, EIGHT_LIST_WINDOW], F32, name="sig_win%d" % t) for t in range(SETS)]
+        for window in y_win + sq_win + sig_win:
             nc.vector.memset(window[:, S:], 0.0)
 
         w1w = keep.tile([P, H], U32, name="w1w", align_bytes=64)
         w1s = keep.tile([P, H], U8, name="w1s", align_bytes=64)
-        nc.vector.tensor_copy(out=dealt(w1s), in_=w1s_raw[:].rearrange("p (m t) -> p m t", t=PACK))
-        nc.scalar.copy(out=dealt(w1w), in_=w1w_raw[:].rearrange("p (m t) -> p m t", t=PACK))
+        nc.vector.tensor_copy(out=dealt(w1s), in_=w1s_raw[:].rearrange("p (m t) -> p m t", t=SETS))
+        for u in range(PAIRS):
+            pair = slice(2 * u, 2 * u + 2)
+            nc.scalar.copy(out=dealt(w1w)[:, :, pair], in_=w1w_raw[:].rearrange("p (m t) -> p m t", t=SETS)[:, :, pair])
 
         xq_w = keep.tile([P, S], U32, name="xq_w", align_bytes=64)
         xq_s = keep.tile([P, S], U8, name="xq_s", align_bytes=64)
         nc.vector.tensor_copy(out=xq_w[:], in_=xw[:].indirect(offs_l[:]))
         nc.vector.tensor_copy(out=xq_s[:], in_=xs[:].indirect(offs_l[:]))
-        y_ps = []
-        for t in range(PACK):
-            y_t = psum.tile([P, S], F32, name="y_ps%d" % t)
+        y_ps = [psum.tile([P, S], F32, name="y_ps%d" % t, tag="low%d" % t) for t in range(SETS)]
+        for t in range(SETS):
             cols = slice(P * t, P * (t + 1))
             nc.tensor.matmul_mx(
-                out=y_t[:], lhsT=w1w[:, cols].bitcast(FP8X4), lhsT_scale=w1s[:, cols],
-                rhs=xq_w[:].bitcast(FP8X4), rhs_scale=xq_s[:], start=True, stop=True,
+                out=y_ps[t][:],
+                lhsT=w1w[:, cols].bitcast(FP8X4),
+                lhsT_scale=w1s[:, cols],
+                rhs=xq_w[:].bitcast(FP8X4),
+                rhs_scale=xq_s[:],
+                start=True,
+                stop=True,
             )
-            y_ps.append(y_t)
 
         def pick(window, dtype, lst, name, tag):
             picked = keep.tile([P, C], dtype, name=name, tag=tag, align_bytes=64)
             nc.vector.tensor_copy(out=dealt(picked), in_=window[:].indirect(lst[:]))
             return picked
 
-        def score(picked, values, name, bank_tag):
-            grouped = keep.tile([P, S, PACK], BF16, name=name + "_bf", align_bytes=64)
+        def score(words, scale_bytes, values, name, bank_tag):
+            grouped = keep.tile([P, S, SETS], BF16, name=name + "_bf", align_bytes=64)
             codes = keep.tile([P, S], U32, name=name + "_codes", align_bytes=64)
             scales = keep.tile([P, S], U8, name=name + "_scales", align_bytes=64)
             interleave(grouped, values)
-            nc.vector.quantize_mx(out=codes[:].bitcast(FP8X4), scales=scales[:], in_=grouped[:].rearrange("p j t -> p (j t)"))
-            banks = [psum.tile([P, S], F32, name="%s_ps%d" % (name, t), tag="%s%d" % (bank_tag, t)) for t in range(PACK)]
-            for t in range(PACK):
+            nc.vector.quantize_mx(
+                out=codes[:].bitcast(FP8X4), scales=scales[:], in_=grouped[:].rearrange("p j t -> p (j t)")
+            )
+            banks = [psum.tile([P, S], F32, name="%s_ps%d" % (name, t), tag="%s%d" % (bank_tag, t)) for t in range(SETS)]
+            for t in range(SETS):
                 cols = slice(P * t, P * (t + 1))
                 nc.tensor.matmul_mx(
-                    out=banks[t][:], lhsT=picked[0][:, cols].bitcast(FP8X4), lhsT_scale=picked[1][:, cols],
-                    rhs=codes[:].bitcast(FP8X4), rhs_scale=scales[:], start=True, stop=True,
+                    out=banks[t][:],
+                    lhsT=words[:, cols].bitcast(FP8X4),
+                    lhsT_scale=scale_bytes[:, cols],
+                    rhs=codes[:].bitcast(FP8X4),
+                    rhs_scale=scales[:],
+                    start=True,
+                    stop=True,
                 )
             return banks
 
-        x_cb = (pick(xw, U32, cb_l, "xcb_w", "xcb_w"), pick(xs, U8, cb_l, "xcb_s", "xcb_s"))
+        xcb_w = pick(xw, U32, cb_l, "xcb_w", "w1s_raw")
+        xcb_s = pick(xs, U8, cb_l, "xcb_s", "xcb_s")
         xca_s = pick(xs, U8, ca_l, "xca_s", "xca_s")
-        nc.scalar.activation(out=sq_w[0][:, :S], in_=y_ps[0][:], func=ACT.Square)
-        nc.scalar.copy(out=y_w[0][:, :S], in_=y_ps[0][:])
-        nc.scalar.activation(out=sq_w[1][:, :S], in_=y_ps[1][:], func=ACT.Square)
-        nc.scalar.copy(out=y_w[1][:, :S], in_=y_ps[1][:])
-        nc.scalar.activation(out=sq_w[2][:, :S], in_=y_ps[2][:], func=ACT.Square)
-        nc.scalar.copy(out=y_w[2][:, :S], in_=y_ps[2][:])
-        nc.scalar.activation(out=sq_w[3][:, :S], in_=y_ps[3][:], func=ACT.Square)
-        nc.scalar.copy(out=y_w[3][:, :S], in_=y_ps[3][:])
-        sq3 = keep.tile([P, PACK, S], F32, name="sq3", align_bytes=64)
-        ssum = keep.tile([P, PACK, S], F32, name="ssum")
-        rinv = keep.tile([P, PACK, S], F32, name="rinv")
-        y4 = keep.tile([P, PACK, S], F32, name="y4")
-        z2 = keep.tile([P, PACK, S], F32, name="z2")
-        tab1 = keep.tile([P, PACK, S], F32, name="tab1")
-        larger = keep.tile([P, PACK, S], F32, name="larger")
-        z = keep.tile([P, PACK, S], F32, name="z")
-        gate = [keep.tile([P, 2, S], F32, name="gate%d" % u) for u in range(2)]
-        gated = keep.tile([P, PACK, S], F32, name="gated")
-        a_w = [keep.tile([P, S], F32, name="a_win%d" % t) for t in range(PACK)]
-        res = [keep.tile([P, PACK, HALF], F32, name="res%d" % h) for h in range(2)]
-        res_bf = [keep.tile([P, HALF, PACK], BF16, name="res_bf%d" % h, align_bytes=64) for h in range(2)]
-        res_codes = keep.tile([P, S], U32, name="res_codes", align_bytes=64)
-        res_scales = keep.tile([P, S], U8, name="res_scales", align_bytes=64)
-        entries = [slice(h * HALF // LIST_COL, (h + 1) * HALF // LIST_COL) for h in range(2)]
-        nc.vector.tensor_copy(out=sq3[:, 0, :], in_=sq_w[0][:].indirect(n3_l[:]))
-        nc.vector.tensor_tensor(out=ssum[:, 0, :], in0=sq3[:, 0, :], in1=sq_w[0][:, :S], op=ALU.add)
-        nc.vector.tensor_copy(out=sq3[:, 1, :], in_=sq_w[1][:].indirect(n3_l[:]))
-        nc.vector.tensor_tensor(out=ssum[:, 1, :], in0=sq3[:, 1, :], in1=sq_w[1][:, :S], op=ALU.add)
-        nc.vector.tensor_copy(out=sq3[:, 2, :], in_=sq_w[2][:].indirect(n3_l[:]))
-        nc.vector.tensor_tensor(out=ssum[:, 2, :], in0=sq3[:, 2, :], in1=sq_w[2][:, :S], op=ALU.add)
-        nc.vector.tensor_copy(out=sq3[:, 3, :], in_=sq_w[3][:].indirect(n3_l[:]))
-        nc.vector.tensor_tensor(out=ssum[:, 3, :], in0=sq3[:, 3, :], in1=sq_w[3][:, :S], op=ALU.add)
-        x_ca = (pick(xw, U32, ca_l, "xca_w", "sq3"), xca_s)
-        for t in range(PACK):
-            nc.scalar.activation(out=y4[:, t, :], in_=y_w[t][:].indirect(n4_l[:]), func=ACT.Copy)
-        for u in range(2):
-            nc.scalar.activation(out=rinv[:, 2 * u : 2 * u + 2, :], in_=ssum[:, 2 * u : 2 * u + 2, :], func=ACT.Abs_reciprocal_sqrt, bias=0.25)
-        for t in range(PACK):
+        for t in range(SETS):
+            nc.scalar.activation(out=sq_win[t][:, :S], in_=y_ps[t][:], func=ACT.Square)
+            nc.scalar.copy(out=y_win[t][:, :S], in_=y_ps[t][:])
+
+        sq3 = keep.tile([P, SETS, S], F32, name="sq3", align_bytes=64)
+        sum_ps = [psum.tile([P, 2, P], F32, name="sum_ps%d" % t, tag="high%d" % t) for t in range(SETS)]
+        root_t = keep.tile([P, SETS, 2, P], F32, name="root_t")
+        root_ps = [psum.tile([P, S], F32, name="root_ps%d" % t, tag="low%d" % t) for t in range(SETS)]
+        y4 = keep.tile([P, SETS, S], F32, name="y4")
+        z2 = keep.tile([P, SETS, S], F32, name="z2")
+        halves = [slice(h * HALF, (h + 1) * HALF) for h in range(2)]
+        for t in range(SETS):
+            nc.vector.tensor_copy(out=sq3[:, t, :], in_=sq_win[t][:].indirect(n3_l[:]))
+            for h, cols in enumerate(halves):
+                nc.tensor.matmul(
+                    out=sum_ps[t][:, h, :], lhsT=sq_win[t][:, cols], rhs=ident[:], is_transpose=True, start=True, stop=False
+                )
+                nc.tensor.matmul(
+                    out=sum_ps[t][:, h, :], lhsT=sq3[:, t, cols], rhs=ident[:], is_transpose=True, start=False, stop=True
+                )
+        xca_w = pick(xw, U32, ca_l, "xca_w", "sq_win%d" % (SETS - 1))
+        for t in range(SETS):
+            nc.scalar.activation(out=y4[:, t, :], in_=y_win[t][:].indirect(n4_l[:]), func=ACT.Copy)
+        for t in range(SETS):
+            nc.scalar.activation(out=root_t[:, t, :, :], in_=sum_ps[t][:], func=ACT.Abs_reciprocal_sqrt, bias=0.25)
+            for h, cols in enumerate(halves):
+                nc.tensor.transpose(root_ps[t][:, cols], root_t[:, t, h, :], ident[:])
+        for t in range(SETS):
             nc.vector.scalar_tensor_tensor(
-                out=z2[:, t, :], in0=y4[:, t, :], scalar=gs2_sb[:, t : t + 1], in1=rinv[:, t, :], op0=ALU.mult, op1=ALU.mult
+                out=z2[:, t, :], in0=y4[:, t, :], scalar=gs2_sb[:, t : t + 1], in1=root_ps[t][:], op0=ALU.mult, op1=ALU.mult
             )
-        b_ps = score(x_cb, z2, "b", "y_ps")
-        first = keep.tile([P, PACK, S], F32, name="first")
-        y2 = [keep.tile([P, 2, S], F32, name="y2_0"), keep.tile([P, 2, S], F32, name="y2_1")]
-        for t in range(PACK):
-            nc.scalar.activation(out=tab1[:, t, :], in_=tab_w[t][:].indirect(n1_l[:]), func=ACT.Copy)
-            nc.vector.tensor_tensor(out=first[:, t, :], in0=y_w[t][:, :S], in1=tab1[:, t, :], op=ALU.add)
-        nc.scalar.activation(out=y2[0][:, 0, :], in_=y_w[0][:].indirect(n2_l[:]), func=ACT.Copy)
-        nc.scalar.activation(out=y2[0][:, 1, :], in_=y_w[1][:].indirect(n2_l[:]), func=ACT.Copy)
-        nc.scalar.activation(out=y2[1][:, 0, :], in_=y_w[2][:].indirect(n2_l[:]), func=ACT.Copy)
-        nc.vector.tensor_copy(out=y2[1][:, 1, :], in_=y_w[3][:].indirect(n2_l[:]))
-        for u in range(2):
+        b_ps = score(xcb_w, xcb_s, z2, "b", "low")
+
+        tab1 = [keep.tile([P, 2, S], F32, name="tab1_0"), keep.tile([P, 2, S], F32, name="tab1_1", tag="sq3", align_bytes=64)]
+        first = keep.tile([P, SETS, S], F32, name="first", tag="b_bf", align_bytes=64)
+        y2 = [keep.tile([P, 2, S], F32, name="y2_0", tag="y4"), keep.tile([P, 2, S], F32, name="y2_1")]
+        larger = keep.tile([P, SETS, S], F32, name="larger")
+        z = keep.tile([P, SETS, S], F32, name="z")
+        for t in range(SETS):
+            nc.scalar.activation(out=tab1[t // 2][:, t % 2, :], in_=tab_win[t][:].indirect(n1_l[:]), func=ACT.Copy)
+            nc.vector.tensor_tensor(out=first[:, t, :], in0=y_win[t][:, :S], in1=tab1[t // 2][:, t % 2, :], op=ALU.add)
+        for t in range(PAIRS):
+            nc.scalar.activation(out=y2[0][:, t, :], in_=y_win[t][:].indirect(n2_l[:]), func=ACT.Copy)
+        for t in range(PAIRS):
+            nc.vector.tensor_copy(out=y2[1][:, t, :], in_=y_win[2 + t][:].indirect(n2_l[:]))
+        for u in range(PAIRS):
             pair = slice(2 * u, 2 * u + 2)
             nc.vector.tensor_tensor(out=larger[:, pair, :], in0=first[:, pair, :], in1=y2[u][:], op=ALU.max)
-        for t in range(PACK):
-            nc.vector.tensor_scalar(out=z[:, t, :], in0=larger[:, t, :], scalar1=gs_sb[:, t : t + 1], scalar2=None, op0=ALU.mult)
-        a_ps = score(x_ca, z, "a", "a_ps")
-        nc.scalar.activation(out=b_w[0][:, :S], in_=b_ps[0][:], func=ACT.Sigmoid, scale=0.0625)
-        nc.scalar.activation(out=b_w[1][:, :S], in_=b_ps[1][:], func=ACT.Sigmoid, scale=0.0625)
-        nc.scalar.activation(out=b_w[2][:, :S], in_=b_ps[2][:], func=ACT.Sigmoid, scale=0.0625)
-        nc.scalar.activation(out=b_w[3][:, :S], in_=b_ps[3][:], func=ACT.Sigmoid, scale=0.0625)
-        for t in range(PACK):
-            nc.scalar.activation(out=gate[t // 2][:, t % 2, :], in_=b_w[t][:].indirect(n6_l[:]), func=ACT.Copy)
-        nc.vector.tensor_scalar(out=a_w[0][:], in0=a_ps[0][:], scalar1=0.0625, scalar2=None, op0=ALU.mult)
-        nc.vector.tensor_scalar(out=a_w[1][:], in0=a_ps[1][:], scalar1=0.0625, scalar2=None, op0=ALU.mult)
-        nc.vector.tensor_scalar(out=a_w[2][:], in0=a_ps[2][:], scalar1=0.0625, scalar2=None, op0=ALU.mult)
-        nc.vector.tensor_scalar(out=a_w[3][:], in0=a_ps[3][:], scalar1=0.0625, scalar2=None, op0=ALU.mult)
-        for t in range(PACK):
-            nc.vector.scalar_tensor_tensor(
-                out=gated[:, t, :], in0=a_ps[t][:], scalar=0.0625, in1=gate[t // 2][:, t % 2, :], op0=ALU.mult, op1=ALU.mult
+        for t in range(SETS):
+            nc.vector.tensor_scalar(
+                out=z[:, t, :], in0=larger[:, t, :], scalar1=gs_sb[:, t : t + 1], scalar2=None, op0=ALU.mult
             )
-        a5 = [keep.tile([P, PACK, HALF], F32, name="a5_0"), keep.tile([P, PACK, HALF], F32, name="a5_1", tag="gate0")]
-        out_rows = out_0.rearrange("(p t) j -> p t j", t=PACK)
-        out_words = out_1[0].rearrange("p n t -> p (n t)").bitcast(I32)
-        for h in range(2):
-            cols = slice(h * HALF, (h + 1) * HALF)
-            for u in range(2):
+        a_ps = score(xca_w, xca_s, z, "a", "high")
+
+        gate = [keep.tile([P, 2, S], F32, name="gate%d" % u) for u in range(PAIRS)]
+        gated = keep.tile([P, SETS, S], F32, name="gated")
+        a_win = [keep.tile([P, S], F32, name="a_win%d" % t) for t in range(SETS)]
+        for t in range(SETS):
+            nc.scalar.activation(out=sig_win[t][:, :S], in_=b_ps[t][:], func=ACT.Sigmoid, scale=SCORE_SCALE)
+        for t in range(SETS):
+            nc.scalar.activation(out=gate[t // 2][:, t % 2, :], in_=sig_win[t][:].indirect(n6_l[:]), func=ACT.Copy)
+        for t in range(SETS):
+            nc.vector.tensor_scalar(out=a_win[t][:], in0=a_ps[t][:], scalar1=SCORE_SCALE, scalar2=None, op0=ALU.mult)
+        for t in range(SETS):
+            nc.vector.scalar_tensor_tensor(
+                out=gated[:, t, :],
+                in0=a_ps[t][:],
+                scalar=SCORE_SCALE,
+                in1=gate[t // 2][:, t % 2, :],
+                op0=ALU.mult,
+                op1=ALU.mult,
+            )
+
+        a5 = [keep.tile([P, SETS, HALF], F32, name="a5_0"), keep.tile([P, SETS, HALF], F32, name="a5_1", tag="gate0")]
+        res = [keep.tile([P, SETS, HALF], F32, name="res%d" % h) for h in range(2)]
+        res_bf = [keep.tile([P, HALF, SETS], BF16, name="res_bf%d" % h, align_bytes=64) for h in range(2)]
+        res_codes = keep.tile([P, S], U32, name="res_codes", align_bytes=64)
+        res_scales = keep.tile([P, S], U8, name="res_scales", align_bytes=64)
+        out_rows = out_0.rearrange("(p t) j -> p t j", t=SETS)
+        out_words = as_words(out_1)
+        for h, cols in enumerate(halves):
+            entries = slice(h * HALF // LIST_ROWS, (h + 1) * HALF // LIST_ROWS)
+            for u in range(PAIRS):
                 pair = slice(2 * u, 2 * u + 2)
                 for t in range(2 * u, 2 * u + 2):
-                    nc.scalar.activation(out=a5[h][:, t, :], in_=a_w[t][:].indirect(n5_l[:, entries[h]]), func=ACT.Copy)
+                    nc.scalar.activation(out=a5[h][:, t, :], in_=a_win[t][:].indirect(n5_l[:, entries]), func=ACT.Copy)
                 nc.vector.scalar_tensor_tensor(
-                    out=res[h][:, pair, :], in0=a5[h][:, pair, :], scalar=-0.5, in1=gated[:, pair, cols], op0=ALU.mult, op1=ALU.add
+                    out=res[h][:, pair, :],
+                    in0=a5[h][:, pair, :],
+                    scalar=-0.5,
+                    in1=gated[:, pair, cols],
+                    op0=ALU.mult,
+                    op1=ALU.add,
                 )
             nc.sync.dma_start(out_rows[:, :, cols], res[h][:])
             interleave(res_bf[h], res[h])
             nc.vector.quantize_mx(
-                out=res_codes[:, cols].bitcast(FP8X4), scales=res_scales[:, cols], in_=res_bf[h][:].rearrange("p j t -> p (j t)")
+                out=res_codes[:, cols].bitcast(FP8X4),
+                scales=res_scales[:, cols],
+                in_=res_bf[h][:].rearrange("p j t -> p (j t)"),
             )
             nc.sync.dma_start(out_words[:, cols], res_codes[:, cols].bitcast(I32))
         for q in range(QUADS):

@@ -101,6 +101,11 @@ def tile_picked_twocdgatebkindrms_none_po_kernel(
         for window in y_win + sq_win + sig_win:
             nc.vector.memset(window[:, S:], 0.0)
 
+        warm_in = keep.tile([P, 1], F32, name="warm_in")
+        warm_out = keep.tile([P, 1], F32, name="warm_out")
+        nc.vector.memset(warm_in[:], 1.0)
+        nc.scalar.activation(out=warm_out[:], in_=warm_in[:], func=ACT.Abs_reciprocal_sqrt)
+
         w1w = keep.tile([P, H], U32, name="w1w", align_bytes=64)
         w1s = keep.tile([P, H], U8, name="w1s", align_bytes=64)
         nc.vector.tensor_copy(out=dealt(w1s), in_=w1s_raw[:].rearrange("p (m t) -> p m t", t=SETS))

@@ -26,6 +26,7 @@ LINE = 4
 ONE_LIST_WINDOW = 352
 EIGHT_LIST_WINDOW = 2 * S
 SCORE_SCALE = 0.0625
+N2_ON_SCALAR = 2
 
 
 def tile_picked_twocdgatebkindrms_none_po_kernel(
@@ -35,6 +36,8 @@ def tile_picked_twocdgatebkindrms_none_po_kernel(
     with ExitStack() as ctx:
         keep = ctx.enter_context(tc.tile_pool(name="keep", bufs=1))
         psum = ctx.enter_context(tc.psum_pool(name="psum", bufs=1))
+
+        halves = [slice(h * HALF, (h + 1) * HALF) for h in range(2)]
 
         def load_list(src, name):
             lst = keep.tile(list(src.shape), U16, name=name)
@@ -55,7 +58,7 @@ def tile_picked_twocdgatebkindrms_none_po_kernel(
 
         def interleave(dst, src):
             nc.vector.tensor_copy(
-                out=dst[:].rearrange("p (c i) t -> p c t i", i=LINE), in_=src[:].rearrange("p t (c i) -> p c t i", i=LINE)
+                out=dst[:].rearrange("p (c i) t -> p c t i", i=LINE), in_=src.rearrange("p t (c i) -> p c t i", i=LINE)
             )
 
         xs = keep.tile([P, T], U8, name="xs", align_bytes=64)
@@ -76,7 +79,7 @@ def tile_picked_twocdgatebkindrms_none_po_kernel(
         for q in range(QUADS // 2, QUADS):
             load_scale_rows(nc.sync, xs, x_scales, q)
         nc.sync.dma_start(xw[:].bitcast(I32), as_words(x_words))
-        for q in range(QUADS):
+        for q in range(1, QUADS):
             load_scale_rows(nc.sync, w1s_raw, w1_scales, q)
         nc.sync.dma_start(w1w_raw[:].bitcast(I32), as_words(w1_words))
         nc.sync.dma_start(tab_win[0][:], tab_rows[:, 0, :])
@@ -94,6 +97,7 @@ def tile_picked_twocdgatebkindrms_none_po_kernel(
         n5_l = load_list(n5, "n5_l")
         for q in range(QUADS // 2):
             load_scale_rows(nc.scalar, xs, x_scales, q)
+        load_scale_rows(nc.scalar, w1s_raw, w1_scales, 0)
 
         y_win = [keep.tile([P, ONE_LIST_WINDOW], F32, name="y_win%d" % t) for t in range(SETS)]
         sq_win = [keep.tile([P, ONE_LIST_WINDOW], F32, name="sq_win%d" % t, align_bytes=64) for t in range(SETS)]
@@ -135,26 +139,30 @@ def tile_picked_twocdgatebkindrms_none_po_kernel(
             nc.vector.tensor_copy(out=dealt(picked), in_=window[:].indirect(lst[:]))
             return picked
 
-        def score(words, scale_bytes, values, name, bank_tag):
-            grouped = keep.tile([P, S, SETS], BF16, name=name + "_bf", align_bytes=64)
+        def score(words, scale_bytes, group, name, bank_tag):
+            grouped = [keep.tile([P, HALF, SETS], BF16, name="%s_bf%d" % (name, h), align_bytes=64) for h in range(2)]
             codes = keep.tile([P, S], U32, name=name + "_codes", align_bytes=64)
             scales = keep.tile([P, S], U8, name=name + "_scales", align_bytes=64)
-            interleave(grouped, values)
-            nc.vector.quantize_mx(
-                out=codes[:].bitcast(FP8X4), scales=scales[:], in_=grouped[:].rearrange("p j t -> p (j t)")
-            )
             banks = [psum.tile([P, S], F32, name="%s_ps%d" % (name, t), tag="%s%d" % (bank_tag, t)) for t in range(SETS)]
-            for t in range(SETS):
-                cols = slice(P * t, P * (t + 1))
-                nc.tensor.matmul_mx(
-                    out=banks[t][:],
-                    lhsT=words[:, cols].bitcast(FP8X4),
-                    lhsT_scale=scale_bytes[:, cols],
-                    rhs=codes[:].bitcast(FP8X4),
-                    rhs_scale=scales[:],
-                    start=True,
-                    stop=True,
+            for h, places in enumerate(halves):
+                group(grouped[h], places)
+            for h, places in enumerate(halves):
+                nc.vector.quantize_mx(
+                    out=codes[:, places].bitcast(FP8X4),
+                    scales=scales[:, places],
+                    in_=grouped[h][:].rearrange("p j t -> p (j t)"),
                 )
+                for t in range(SETS):
+                    cols = slice(P * t, P * (t + 1))
+                    nc.tensor.matmul_mx(
+                        out=banks[t][:, places],
+                        lhsT=words[:, cols].bitcast(FP8X4),
+                        lhsT_scale=scale_bytes[:, cols],
+                        rhs=codes[:, places].bitcast(FP8X4),
+                        rhs_scale=scales[:, places],
+                        start=True,
+                        stop=True,
+                    )
             return banks
 
         xcb_w = pick(xw, U32, cb_l, "xcb_w", "w1s_raw")
@@ -170,7 +178,6 @@ def tile_picked_twocdgatebkindrms_none_po_kernel(
         root_ps = [psum.tile([P, S], F32, name="root_ps%d" % t, tag="low%d" % t) for t in range(SETS)]
         y4 = keep.tile([P, SETS, S], F32, name="y4")
         z2 = keep.tile([P, SETS, S], F32, name="z2")
-        halves = [slice(h * HALF, (h + 1) * HALF) for h in range(2)]
         for t in range(SETS):
             nc.vector.tensor_copy(out=sq3[:, t, :], in_=sq_win[t][:].indirect(n3_l[:]))
             for h, cols in enumerate(halves):
@@ -191,28 +198,33 @@ def tile_picked_twocdgatebkindrms_none_po_kernel(
             nc.vector.scalar_tensor_tensor(
                 out=z2[:, t, :], in0=y4[:, t, :], scalar=gs2_sb[:, t : t + 1], in1=root_ps[t][:], op0=ALU.mult, op1=ALU.mult
             )
-        b_ps = score(xcb_w, xcb_s, z2, "b", "low")
+        b_ps = score(xcb_w, xcb_s, lambda dst, places: interleave(dst, z2[:, :, places]), "b", "low")
 
         tab1 = [keep.tile([P, 2, S], F32, name="tab1_0"), keep.tile([P, 2, S], F32, name="tab1_1", tag="sq3", align_bytes=64)]
-        first = keep.tile([P, SETS, S], F32, name="first", tag="b_bf", align_bytes=64)
-        y2 = [keep.tile([P, 2, S], F32, name="y2_0", tag="y4"), keep.tile([P, 2, S], F32, name="y2_1")]
+        first = keep.tile([P, SETS, S], F32, name="first", tag="b_bf1", align_bytes=64)
+        shares = [slice(0, N2_ON_SCALAR), slice(N2_ON_SCALAR, SETS)]
+        y2_s = keep.tile([P, N2_ON_SCALAR, S], F32, name="y2_s", tag="y4")
+        y2_v = keep.tile([P, SETS - N2_ON_SCALAR, S], F32, name="y2_v")
         larger = keep.tile([P, SETS, S], F32, name="larger")
-        z = keep.tile([P, SETS, S], F32, name="z")
         for t in range(SETS):
             nc.scalar.activation(out=tab1[t // 2][:, t % 2, :], in_=tab_win[t][:].indirect(n1_l[:]), func=ACT.Copy)
             nc.vector.tensor_tensor(out=first[:, t, :], in0=y_win[t][:, :S], in1=tab1[t // 2][:, t % 2, :], op=ALU.add)
-        for t in range(PAIRS):
-            nc.scalar.activation(out=y2[0][:, t, :], in_=y_win[t][:].indirect(n2_l[:]), func=ACT.Copy)
-        for t in range(PAIRS):
-            nc.vector.tensor_copy(out=y2[1][:, t, :], in_=y_win[2 + t][:].indirect(n2_l[:]))
-        for u in range(PAIRS):
-            pair = slice(2 * u, 2 * u + 2)
-            nc.vector.tensor_tensor(out=larger[:, pair, :], in0=first[:, pair, :], in1=y2[u][:], op=ALU.max)
-        for t in range(SETS):
-            nc.vector.tensor_scalar(
-                out=z[:, t, :], in0=larger[:, t, :], scalar1=gs_sb[:, t : t + 1], scalar2=None, op0=ALU.mult
+        for t in range(N2_ON_SCALAR):
+            nc.scalar.activation(out=y2_s[:, t, :], in_=y_win[t][:].indirect(n2_l[:]), func=ACT.Copy)
+        for t in range(N2_ON_SCALAR, SETS):
+            nc.vector.tensor_copy(out=y2_v[:, t - N2_ON_SCALAR, :], in_=y_win[t][:].indirect(n2_l[:]))
+        for share, y2 in zip(shares, (y2_s, y2_v)):
+            nc.vector.tensor_tensor(out=larger[:, share, :], in0=first[:, share, :], in1=y2[:], op=ALU.max)
+
+        def weigh_and_interleave(dst, places):
+            nc.vector.tensor_tensor(
+                out=dst[:].rearrange("p (c i) t -> p c t i", i=LINE),
+                in0=larger[:, :, places].rearrange("p t (c i) -> p c t i", i=LINE),
+                in1=gs_sb[:].rearrange("p (c t i) -> p c t i", c=1, i=1).to_broadcast([P, HALF // LINE, SETS, LINE]),
+                op=ALU.mult,
             )
-        a_ps = score(xca_w, xca_s, z, "a", "high")
+
+        a_ps = score(xca_w, xca_s, weigh_and_interleave, "a", "high")
 
         gate = [keep.tile([P, 2, S], F32, name="gate%d" % u) for u in range(PAIRS)]
         gated = keep.tile([P, SETS, S], F32, name="gated")
@@ -255,7 +267,7 @@ def tile_picked_twocdgatebkindrms_none_po_kernel(
                     op1=ALU.add,
                 )
             nc.sync.dma_start(out_rows[:, :, cols], res[h][:])
-            interleave(res_bf[h], res[h])
+            interleave(res_bf[h], res[h][:])
             nc.vector.quantize_mx(
                 out=res_codes[:, cols].bitcast(FP8X4),
                 scales=res_scales[:, cols],

from contextlib import ExitStack

import concourse.mybir as mybir
from concourse.masks import make_identity

K, T, S, H, J, C = 512, 2048, 256, 512, 512, 512
FLOPS = 2 * K * H * S + 2 * 2 * K * C * S

F32 = mybir.dt.float32
BF16 = mybir.dt.bfloat16
I32 = mybir.dt.int32
U32 = mybir.dt.uint32
U16 = mybir.dt.uint16
U8 = mybir.dt.uint8
FP8X4 = mybir.dt.float8_e4m3fn_x4
ALU = mybir.AluOpType
ACT = mybir.ActivationFunctionType

P = 128
SETS = 4
PAIRS = SETS // 2
QUADS = 4
HALF = S // 2
LIST_ROWS = 16
LINE = 4
ONE_LIST_WINDOW = 352
EIGHT_LIST_WINDOW = 2 * S
SCORE_SCALE = 0.0625
N2_ON_SCALAR = 2


def tile_picked_twocdgatebkindrms_none_po_kernel(
    tc, x_words, x_scales, w1_words, w1_scales, tab, gs, gs2, offs, n1, n2, n3, n4, ca, cb, n5, n6, out_0, out_1, out_2
):
    nc = tc.nc
    with ExitStack() as ctx:
        keep = ctx.enter_context(tc.tile_pool(name="keep", bufs=1))
        psum = ctx.enter_context(tc.psum_pool(name="psum", bufs=1))

        halves = [slice(h * HALF, (h + 1) * HALF) for h in range(2)]

        def load_list(src, name):
            lst = keep.tile(list(src.shape), U16, name=name)
            nc.sync.dma_start(lst[:], src)
            return lst

        def load_scale_rows(queue, scale_tile, src, q):
            queue.dma_start(scale_tile[32 * q : 32 * q + 4, :].bitcast(I32), src[0, 4 * q : 4 * q + 4, :].bitcast(I32))

        def as_words(packed):
            return packed[0].rearrange("p n t -> p (n t)").bitcast(I32)

        def by_set(column):
            return column.rearrange("(p t) o -> p (t o)", t=SETS)

        def dealt(tile):
            return tile[:].rearrange("p (t m) -> p m t", t=SETS)

        def interleave(dst, src):
            nc.vector.tensor_copy(
                out=dst[:].rearrange("p (c i) t -> p c t i", i=LINE), in_=src.rearrange("p t (c i) -> p c t i", i=LINE)
            )

        xs = keep.tile([P, T], U8, name="xs", align_bytes=64)
        w1s_raw = keep.tile([P, H], U8, name="w1s_raw", align_bytes=64)
        nc.gpsimd.memset(xs[:].bitcast(I32), 0)
        nc.gpsimd.memset(w1s_raw[:].bitcast(I32), 0)
        ident = keep.tile([P, P], F32, name="ident")
        make_identity(nc, ident[:])

        xw = keep.tile([P, T], U32, name="xw", align_bytes=64)
        w1w_raw = keep.tile([P, H], U32, name="w1w_raw", align_bytes=64)
        tab_rows = tab.rearrange("(p t) j -> p t j", t=SETS)
        tab_win = [keep.tile([P, J], F32, name="tab_win%d" % t) for t in range(SETS)]
        gs_sb = keep.tile([P, SETS], F32, name="gs_sb")
        gs2_sb = keep.tile([P, SETS], F32, name="gs2_sb")
        offs_l = load_list(offs, "offs_l")
        cb_l = load_list(cb, "cb_l")
        for q in range(QUADS // 2, QUADS):
            load_scale_rows(nc.sync, xs, x_scales, q)
        nc.sync.dma_start(xw[:].bitcast(I32), as_words(x_words))
        for q in range(1, QUADS):
            load_scale_rows(nc.sync, w1s_raw, w1_scales, q)
        nc.sync.dma_start(w1w_raw[:].bitcast(I32), as_words(w1_words))
        nc.sync.dma_start(tab_win[0][:], tab_rows[:, 0, :])
        n1_l = load_list(n1, "n1_l")
        ca_l = load_list(ca, "ca_l")
        n3_l = load_list(n3, "n3_l")
        n4_l = load_list(n4, "n4_l")
        nc.sync.dma_start(tab_win[1][:], tab_rows[:, 1, :])
        n2_l = load_list(n2, "n2_l")
        nc.sync.dma_start(gs2_sb[:], by_set(gs2))
        for t in range(PAIRS, SETS):
            nc.sync.dma_start(tab_win[t][:], tab_rows[:, t, :])
        nc.sync.dma_start(gs_sb[:], by_set(gs))
        n6_l = load_list(n6, "n6_l")
        n5_l = load_list(n5, "n5_l")
        for q in range(QUADS // 2):
            load_scale_rows(nc.scalar, xs, x_scales, q)
        load_scale_rows(nc.scalar, w1s_raw, w1_scales, 0)

        y_win = [keep.tile([P, ONE_LIST_WINDOW], F32, name="y_win%d" % t) for t in range(SETS)]
        sq_win = [keep.tile([P, ONE_LIST_WINDOW], F32, name="sq_win%d" % t, align_bytes=64) for t in range(SETS)]
        sig_win = [keep.tile([P, EIGHT_LIST_WINDOW], F32, name="sig_win%d" % t) for t in range(SETS)]
        for window in y_win + sq_win + sig_win:
            nc.vector.memset(window[:, S:], 0.0)

        warm_in = keep.tile([P, 1], F32, name="warm_in")
        warm_out = keep.tile([P, 1], F32, name="warm_out")
        nc.vector.memset(warm_in[:], 1.0)
        nc.scalar.activation(out=warm_out[:], in_=warm_in[:], func=ACT.Abs_reciprocal_sqrt)

        w1w = keep.tile([P, H], U32, name="w1w", align_bytes=64)
        w1s = keep.tile([P, H], U8, name="w1s", align_bytes=64)
        nc.vector.tensor_copy(out=dealt(w1s), in_=w1s_raw[:].rearrange("p (m t) -> p m t", t=SETS))
        for u in range(PAIRS):
            pair = slice(2 * u, 2 * u + 2)
            nc.scalar.copy(out=dealt(w1w)[:, :, pair], in_=w1w_raw[:].rearrange("p (m t) -> p m t", t=SETS)[:, :, pair])

        xq_w = keep.tile([P, S], U32, name="xq_w", align_bytes=64)
        xq_s = keep.tile([P, S], U8, name="xq_s", align_bytes=64)
        nc.vector.tensor_copy(out=xq_w[:], in_=xw[:].indirect(offs_l[:]))
        nc.vector.tensor_copy(out=xq_s[:], in_=xs[:].indirect(offs_l[:]))
        y_ps = [psum.tile([P, S], F32, name="y_ps%d" % t, tag="low%d" % t) for t in range(SETS)]
        for t in range(SETS):
            cols = slice(P * t, P * (t + 1))
            nc.tensor.matmul_mx(
                out=y_ps[t][:],
                lhsT=w1w[:, cols].bitcast(FP8X4),
                lhsT_scale=w1s[:, cols],
                rhs=xq_w[:].bitcast(FP8X4),
                rhs_scale=xq_s[:],
                start=True,
                stop=True,
            )

        def pick(window, dtype, lst, name, tag):
            picked = keep.tile([P, C], dtype, name=name, tag=tag, align_bytes=64)
            nc.vector.tensor_copy(out=dealt(picked), in_=window[:].indirect(lst[:]))
            return picked

        def score(words, scale_bytes, group, name, bank_tag):
            grouped = [keep.tile([P, HALF, SETS], BF16, name="%s_bf%d" % (name, h), align_bytes=64) for h in range(2)]
            codes = keep.tile([P, S], U32, name=name + "_codes", align_bytes=64)
            scales = keep.tile([P, S], U8, name=name + "_scales", align_bytes=64)
            banks = [psum.tile([P, S], F32, name="%s_ps%d" % (name, t), tag="%s%d" % (bank_tag, t)) for t in range(SETS)]
            for h, places in enumerate(halves):
                group(grouped[h], places)
            for h, places in enumerate(halves):
                nc.vector.quantize_mx(
                    out=codes[:, places].bitcast(FP8X4),
                    scales=scales[:, places],
                    in_=grouped[h][:].rearrange("p j t -> p (j t)"),
                )
                for t in range(SETS):
                    cols = slice(P * t, P * (t + 1))
                    nc.tensor.matmul_mx(
                        out=banks[t][:, places],
                        lhsT=words[:, cols].bitcast(FP8X4),
                        lhsT_scale=scale_bytes[:, cols],
                        rhs=codes[:, places].bitcast(FP8X4),
                        rhs_scale=scales[:, places],
                        start=True,
                        stop=True,
                    )
            return banks

        xcb_w = pick(xw, U32, cb_l, "xcb_w", "w1s_raw")
        xcb_s = pick(xs, U8, cb_l, "xcb_s", "xcb_s")
        xca_s = pick(xs, U8, ca_l, "xca_s", "xca_s")
        for t in range(SETS):
            nc.scalar.activation(out=sq_win[t][:, :S], in_=y_ps[t][:], func=ACT.Square)
            nc.scalar.copy(out=y_win[t][:, :S], in_=y_ps[t][:])

        sq3 = keep.tile([P, SETS, S], F32, name="sq3", align_bytes=64)
        sum_ps = [psum.tile([P, 2, P], F32, name="sum_ps%d" % t, tag="high%d" % t) for t in range(SETS)]
        root_t = keep.tile([P, SETS, 2, P], F32, name="root_t")
        root_ps = [psum.tile([P, S], F32, name="root_ps%d" % t, tag="low%d" % t) for t in range(SETS)]
        y4 = keep.tile([P, SETS, S], F32, name="y4")
        z2 = keep.tile([P, SETS, S], F32, name="z2")
        for t in range(SETS):
            nc.vector.tensor_copy(out=sq3[:, t, :], in_=sq_win[t][:].indirect(n3_l[:]))
            for h, cols in enumerate(halves):
                nc.tensor.matmul(
                    out=sum_ps[t][:, h, :], lhsT=sq_win[t][:, cols], rhs=ident[:], is_transpose=True, start=True, stop=False
                )
                nc.tensor.matmul(
                    out=sum_ps[t][:, h, :], lhsT=sq3[:, t, cols], rhs=ident[:], is_transpose=True, start=False, stop=True
                )
        xca_w = pick(xw, U32, ca_l, "xca_w", "sq_win%d" % (SETS - 1))
        for t in range(SETS):
            nc.scalar.activation(out=y4[:, t, :], in_=y_win[t][:].indirect(n4_l[:]), func=ACT.Copy)
        for t in range(SETS):
            nc.scalar.activation(out=root_t[:, t, :, :], in_=sum_ps[t][:], func=ACT.Abs_reciprocal_sqrt, bias=0.25)
            for h, cols in enumerate(halves):
                nc.tensor.transpose(root_ps[t][:, cols], root_t[:, t, h, :], ident[:])
        for t in range(SETS):
            nc.vector.scalar_tensor_tensor(
                out=z2[:, t, :], in0=y4[:, t, :], scalar=gs2_sb[:, t : t + 1], in1=root_ps[t][:], op0=ALU.mult, op1=ALU.mult
            )
        b_ps = score(xcb_w, xcb_s, lambda dst, places: interleave(dst, z2[:, :, places]), "b", "low")

        tab1 = [keep.tile([P, 2, S], F32, name="tab1_0"), keep.tile([P, 2, S], F32, name="tab1_1", tag="sq3", align_bytes=64)]
        first = keep.tile([P, SETS, S], F32, name="first", tag="b_bf1", align_bytes=64)
        shares = [slice(0, N2_ON_SCALAR), slice(N2_ON_SCALAR, SETS)]
        y2_s = keep.tile([P, N2_ON_SCALAR, S], F32, name="y2_s", tag="y4")
        y2_v = keep.tile([P, SETS - N2_ON_SCALAR, S], F32, name="y2_v")
        larger = keep.tile([P, SETS, S], F32, name="larger")
        for t in range(SETS):
            nc.scalar.activation(out=tab1[t // 2][:, t % 2, :], in_=tab_win[t][:].indirect(n1_l[:]), func=ACT.Copy)
            nc.vector.tensor_tensor(out=first[:, t, :], in0=y_win[t][:, :S], in1=tab1[t // 2][:, t % 2, :], op=ALU.add)
        for t in range(N2_ON_SCALAR):
            nc.scalar.activation(out=y2_s[:, t, :], in_=y_win[t][:].indirect(n2_l[:]), func=ACT.Copy)
        for t in range(N2_ON_SCALAR, SETS):
            nc.vector.tensor_copy(out=y2_v[:, t - N2_ON_SCALAR, :], in_=y_win[t][:].indirect(n2_l[:]))
        for share, y2 in zip(shares, (y2_s, y2_v)):
            nc.vector.tensor_tensor(out=larger[:, share, :], in0=first[:, share, :], in1=y2[:], op=ALU.max)

        def weigh_and_interleave(dst, places):
            nc.vector.tensor_tensor(
                out=dst[:].rearrange("p (c i) t -> p c t i", i=LINE),
                in0=larger[:, :, places].rearrange("p t (c i) -> p c t i", i=LINE),
                in1=gs_sb[:].rearrange("p (c t i) -> p c t i", c=1, i=1).to_broadcast([P, HALF // LINE, SETS, LINE]),
                op=ALU.mult,
            )

        a_ps = score(xca_w, xca_s, weigh_and_interleave, "a", "high")

        gate = [keep.tile([P, 2, S], F32, name="gate%d" % u) for u in range(PAIRS)]
        gated = keep.tile([P, SETS, S], F32, name="gated")
        a_win = [keep.tile([P, S], F32, name="a_win%d" % t) for t in range(SETS)]
        for t in range(SETS):
            nc.scalar.activation(out=sig_win[t][:, :S], in_=b_ps[t][:], func=ACT.Sigmoid, scale=SCORE_SCALE)
        for t in range(SETS):
            nc.scalar.activation(out=gate[t // 2][:, t % 2, :], in_=sig_win[t][:].indirect(n6_l[:]), func=ACT.Copy)
        for t in range(SETS):
            nc.vector.tensor_scalar(out=a_win[t][:], in0=a_ps[t][:], scalar1=SCORE_SCALE, scalar2=None, op0=ALU.mult)
        for t in range(SETS):
            nc.vector.scalar_tensor_tensor(
                out=gated[:, t, :],
                in0=a_ps[t][:],
                scalar=SCORE_SCALE,
                in1=gate[t // 2][:, t % 2, :],
                op0=ALU.mult,
                op1=ALU.mult,
            )

        a5 = [keep.tile([P, SETS, HALF], F32, name="a5_0"), keep.tile([P, SETS, HALF], F32, name="a5_1", tag="gate0")]
        res = [keep.tile([P, SETS, HALF], F32, name="res%d" % h) for h in range(2)]
        res_bf = [keep.tile([P, HALF, SETS], BF16, name="res_bf%d" % h, align_bytes=64) for h in range(2)]
        res_codes = keep.tile([P, S], U32, name="res_codes", align_bytes=64)
        res_scales = keep.tile([P, S], U8, name="res_scales", align_bytes=64)
        out_rows = out_0.rearrange("(p t) j -> p t j", t=SETS)
        out_words = as_words(out_1)
        for h, cols in enumerate(halves):
            entries = slice(h * HALF // LIST_ROWS, (h + 1) * HALF // LIST_ROWS)
            for u in range(PAIRS):
                pair = slice(2 * u, 2 * u + 2)
                for t in range(2 * u, 2 * u + 2):
                    nc.scalar.activation(out=a5[h][:, t, :], in_=a_win[t][:].indirect(n5_l[:, entries]), func=ACT.Copy)
                nc.vector.scalar_tensor_tensor(
                    out=res[h][:, pair, :],
                    in0=a5[h][:, pair, :],
                    scalar=-0.5,
                    in1=gated[:, pair, cols],
                    op0=ALU.mult,
                    op1=ALU.add,
                )
            nc.sync.dma_start(out_rows[:, :, cols], res[h][:])
            interleave(res_bf[h], res[h][:])
            nc.vector.quantize_mx(
                out=res_codes[:, cols].bitcast(FP8X4),
                scales=res_scales[:, cols],
                in_=res_bf[h][:].rearrange("p j t -> p (j t)"),
            )
            nc.sync.dma_start(out_words[:, cols], res_codes[:, cols].bitcast(I32))
        for q in range(QUADS):
            queue = nc.scalar if q % 2 else nc.sync
            queue.dma_start(out_2[0, 4 * q : 4 * q + 4, :].bitcast(I32), res_scales[32 * q : 32 * q + 4, :].bitcast(I32))
